import numpy as np
import ml_dtypes


def mxq(x, axis, fmt="e4m3"):
    dtype, down = {"e4m3": (ml_dtypes.float8_e4m3fn, 7), "e5m2": (ml_dtypes.float8_e5m2, 14)}[fmt]
    v = np.moveaxis(np.asarray(x, np.float32).astype(ml_dtypes.bfloat16).astype(np.float64), axis, -1)
    blocks = v.reshape(v.shape[:-1] + (-1, 32))
    amax = np.abs(blocks).max(-1, keepdims=True)
    byte = np.maximum(np.where(amax > 0, np.frexp(amax)[1] - 1 + 127, 0) - down, 1)
    scale = np.exp2(byte - 127.0)
    codes = (blocks / scale).astype(np.float32).astype(dtype).astype(np.float64)
    return np.moveaxis((codes * scale).reshape(v.shape), -1, axis)


WIDE = False


def mx_kscale(k):
    if not WIDE:
        return np.ones(k)
    levels = np.array([10, -10, 5, -5, 0])
    if k % 512:
        return np.exp2(np.random.permutation(np.resize(levels, k // 32))).repeat(32)
    a = np.empty((k // 512, 16))
    for p in range(k // 512):
        a[p, :8] = np.random.permutation(np.resize(levels, 8))
        for g in range(8):
            far = levels[np.abs(levels - a[p, g]) >= 10]
            a[p, g + 8] = far[np.random.randint(len(far))]
    return np.exp2(a.ravel()).repeat(32)


def f64(x):
    return np.asarray(x).astype(np.float64)


def striped(idx):
    return np.tile(np.asarray(idx).reshape(-1, 16).T, (8, 1)).astype(np.uint16)


def unstriped(offs):
    return offs[:16].T.reshape(-1).astype(np.int64)


E2M1 = np.array([0.0, 0.5, 1.0, 1.5, 2.0, 3.0, 4.0, 6.0, -0.0, -0.5, -1.0, -1.5, -2.0, -3.0, -4.0, -6.0])


def pack_weight(w, fmt):
    k, n = w.shape
    w = f64(np.asarray(w, np.float32).astype(ml_dtypes.bfloat16)).reshape(k // 32, 32, n)
    amax = np.abs(w).max(1)
    if fmt == "e4m3":
        byte = np.frexp(amax)[1] - 1 + 127 - 7
    else:
        mant, ex = np.frexp(amax / 6.0)
        byte = np.where(mant > 0.5, ex, ex - 1) + 127
    byte = np.clip(np.where(amax > 0, byte, 1), 1, 254)
    scaled = (w * np.exp2(127.0 - byte)[:, None, :]).reshape(k, n).astype(np.float32)
    by_word = np.ascontiguousarray(scaled.reshape(k // 512, 128, 4, n).transpose(0, 1, 3, 2))
    if fmt == "e4m3":
        words = by_word.astype(ml_dtypes.float8_e4m3fn).view(np.uint8)
    else:
        c = by_word.astype(ml_dtypes.float4_e2m1fn).view(np.uint8) & 0xF
        words = (c[..., 0::2] | (c[..., 1::2] << 4)).reshape(k // 512, 128, 2 * n)
    return np.ascontiguousarray(words), np.ascontiguousarray(byte.astype(np.uint8).reshape(k // 512, 16, n))


def unpack_weight(words, scales, fmt):
    g, _, n = scales.shape
    words = np.ascontiguousarray(words).reshape(g, 128, n, -1)
    if fmt == "e4m3":
        vals = words.view(ml_dtypes.float8_e4m3fn).astype(np.float64)
    else:
        nib = np.empty((g, 128, n, 4), np.uint8)
        nib[..., 0::2] = words & 0xF
        nib[..., 1::2] = words >> 4
        vals = E2M1[nib]
    vals = vals * np.repeat(np.exp2(scales.astype(np.float64) - 127.0), 8, axis=1)[..., None]
    return vals.transpose(0, 1, 3, 2).reshape(g * 512, n)


def sigmoid(v):
    return 1.0 / (1.0 + np.exp(-v))


D, K, R, T, I, Q, G = 512, 512, 512, 2048, 512, 128, 64


def setup_inputs():
    n = np.random.standard_normal
    idx = np.random.permutation(T)[:I]
    fd = mx_kscale(D)
    fk = mx_kscale(K)
    fr = mx_kscale(R)
    keysp = pack_weight(n((D, T)) / fd[:, None], "e2m1")
    tabp = pack_weight(n((K, T)) / fk[:, None], "e2m1")
    return {
        "query": (n((D, Q)) * 0.6 / np.sqrt(D) * fd[:, None]).astype(np.float32),
        "query2": (n((D, Q)) * 1.0 / np.sqrt(D) * fd[:, None]).astype(np.float32),
        "keys_words": keysp[0],
        "keys_scales": keysp[1],
        "tab_words": tabp[0],
        "tab_scales": tabp[1],
        "w1": (n((K, R)) * 1 / np.sqrt(K) * fk[:, None]).astype(np.float32),
        "temper": (np.random.uniform(0.4, 1.0, (R, 1))).astype(np.float32),
        "gout": (n((R, Q)) * 1 / np.sqrt(R) * fr[:, None]).astype(np.float32),
        "hsc": (np.random.uniform(0.7, 1.4, (R, 1)) / fr[:, None]).astype(np.float32),
        "old": (0.5 * n((Q, T))).astype(np.float32),
        "offs": striped(idx),
    }


def reference(query, query2, keys_words, keys_scales, tab_words, tab_scales, w1, temper, gout, hsc, old, offs):
    idx = unstriped(offs)
    keysu = unpack_weight(keys_words, keys_scales, "e2m1")
    tabu = unpack_weight(tab_words, tab_scales, "e2m1")
    queryq = mxq(f64(query), 0, "e4m3")
    keysidxg = keysu[:, idx]
    a = queryq.T @ keysidxg
    query2q = mxq(f64(query2), 0, "e4m3")
    b = query2q.T @ keysidxg
    p = np.exp(a - np.max(a, axis=1, keepdims=True)) * sigmoid(b)
    z = np.sum(p, axis=1, keepdims=True)
    w1q = mxq(f64(w1), 0, "e4m3")
    tabidxg = tabu[:, idx]
    zh = w1q.T @ tabidxg
    ht = np.exp(zh * f64(temper))
    mz = ht.reshape(R, G, I // G).sum(axis=2)
    mzr = np.repeat(mz, I // G, axis=1)
    hv = ht / mzr * 4.0
    hs1 = hv * f64(hsc)
    goutq = mxq(f64(gout), 0, "e4m3")
    hs1q = mxq(hs1, 0, "e4m3")
    c0 = goutq.T @ hs1q
    dz = np.sum(c0 * p / np.square(z) * (-1.0), axis=1, keepdims=True)
    dp = c0 / z + dz
    da = dp * sigmoid(b) * np.exp(a - np.max(a, axis=1, keepdims=True))
    gs = da * 512.0
    gf = np.zeros((Q, T))
    gf[:, idx] = gs
    y = f64(old) + gf
    return y

@@ -1,0 +1,228 @@
+from contextlib import ExitStack
+
+import concourse.mybir as mybir
+from concourse.masks import make_identity
+
+D, K, R, T, I, Q = 512, 512, 512, 2048, 512, 128
+FLOPS = 2 * I * (2 * D * Q + K * R + R * Q)
+
+F32 = mybir.dt.float32
+BF16 = mybir.dt.bfloat16
+I32 = mybir.dt.int32
+U32 = mybir.dt.uint32
+U16 = mybir.dt.uint16
+U8 = mybir.dt.uint8
+FP8X4 = mybir.dt.float8_e4m3fn_x4
+FP4X4 = mybir.dt.float4_e2m1fn_x4
+ALU = mybir.AluOpType
+ACT = mybir.ActivationFunctionType
+AX = mybir.AxisListType
+
+P = 128
+PACK = 4
+GROUP = 8
+HALVES = 2
+HALF = I // HALVES
+RUN = 4
+RUNS = HALF // GROUP // RUN
+W_SCALAR = 24
+STORE_WIDTHS = (512, 512, 512, 512)
+
+
+def load_scale_rows(queue, plane, scales):
+    rows = scales[0].bitcast(I32).rearrange("(q r) c -> r q c", r=PACK)
+    for r in range(PACK):
+        queue.dma_start(out=plane[r:P:32, :].bitcast(I32), in_=rows[r])
+
+
+def tile_attend_blrshared_asked_kernel(tc, query, query2, keys_words, keys_scales, tab_words, tab_scales,
+                                        w1, temper, gout, hsc, old, offs, out):
+    nc = tc.nc
+    with ExitStack() as ctx:
+        sb = ctx.enter_context(tc.tile_pool(name="sb", bufs=1))
+        ps = ctx.enter_context(tc.psum_pool(name="ps", bufs=1))
+
+        def sbuf(name, shape, dtype, tag=""):
+            return sb.tile(shape, dtype, name=name, tag=tag or name, align_bytes=64)
+
+        def bank(name, tag):
+            return ps.tile([P, 512], F32, name=name, tag=tag)
+
+        offsets = sb.tile([P, I // 16], U16, name="offsets")
+        tab_plane = sbuf("tab_plane", [P, T], U8)
+        placed = sbuf("placed", [P, T], F32)
+        nc.vector.memset(tab_plane[:].bitcast(I32), 0)
+        nc.vector.memset(placed[:], 0.0)
+
+        w_rows = w1.rearrange("(p j) c -> p j c", j=PACK)
+        w_raw = [sbuf("w_raw%d" % u, [P, PACK, R // 2], F32) for u in range(2)]
+        tab_pool = sbuf("tab_pool", [P, T], U16)
+        keys_pool = sbuf("keys_pool", [P, T], U16)
+        q_raw = [sbuf("q_raw%d" % u, [P, PACK, Q], F32) for u in range(3)]
+        temper_t = sbuf("temper_t", [P, PACK], F32)
+        hsc_t = sbuf("hsc_t", [P, PACK], F32)
+        result = sbuf("result", [P, T], F32)
+
+        nc.sync.dma_start(offsets[:], offs)
+        nc.sync.dma_start(out=w_raw[0][:], in_=w_rows[:, :, 0:R // 2])
+        load_scale_rows(nc.sync, tab_plane, tab_scales)
+        nc.sync.dma_start(out=tab_pool[:].bitcast(I32), in_=tab_words[0].bitcast(I32))
+        nc.sync.dma_start(out=w_raw[1][:], in_=w_rows[:, :, R // 2:R])
+        nc.sync.dma_start(out=q_raw[0][:], in_=query.rearrange("(p j) q -> p j q", j=PACK))
+        nc.sync.dma_start(out=q_raw[1][:], in_=query2.rearrange("(p j) q -> p j q", j=PACK))
+        nc.sync.dma_start(out=keys_pool[:].bitcast(I32), in_=keys_words[0].bitcast(I32))
+        nc.sync.dma_start(out=q_raw[2][:], in_=gout.rearrange("(p j) q -> p j q", j=PACK))
+        nc.sync.dma_start(out=result[:], in_=old)
+        nc.gpsimd.dma_start(out=temper_t[:], in_=temper.rearrange("(p t) o -> p (t o)", t=PACK))
+        nc.gpsimd.dma_start(out=hsc_t[:], in_=hsc.rearrange("(p t) o -> p (t o)", t=PACK))
+
+        identity = sbuf("identity", [P, P], F32)
+        make_identity(nc, identity[:])
+
+        w_bf = sbuf("w_bf", [P, PACK, P, PACK], BF16)
+        M2 = P // 2
+
+        def w_views(u, m0, m1):
+            return (w_bf[:, :, u * M2 + m0:u * M2 + m1, :].rearrange("p t m j -> p m t j"),
+                    w_raw[u][:, :, PACK * m0:PACK * m1].rearrange("p j (m t) -> p m t j", t=PACK))
+
+        nc.scalar.activation(*w_views(0, 0, M2), ACT.Copy)
+        keys_plane = sbuf("keys_plane", [P, T], U8, "w_raw0")
+        nc.gpsimd.memset(keys_plane[:].bitcast(I32), 0)
+        load_scale_rows(nc.scalar, keys_plane, keys_scales)
+        tab_sc = sbuf("tab_sc", [P, I], U8)
+        tab_g = sbuf("tab_g", [P, I], U16)
+        nc.vector.tensor_copy(tab_sc[:], tab_plane[:].indirect(offsets[:]))
+        for h in range(HALVES):
+            nc.vector.tensor_copy(tab_g[:, h * HALF:(h + 1) * HALF],
+                                  tab_pool[:].indirect(offsets[:, h * HALF // 16:(h + 1) * HALF // 16]))
+        nc.scalar.activation(*w_views(1, 0, W_SCALAR), ACT.Copy)
+        nc.vector.tensor_copy(*w_views(1, W_SCALAR, M2))
+        w_codes = sbuf("w_codes", [P, R], U32)
+        w_sc = sbuf("w_sc", [P, R], U8)
+        for t in range(PACK):
+            mc = slice(t * P, (t + 1) * P)
+            nc.vector.quantize_mx(out=w_codes[:, mc].bitcast(FP8X4), scales=w_sc[:, mc],
+                                  in_=w_bf[:, t].rearrange("p m j -> p (m j)"))
+
+        q_bf = [sbuf("q_bf%d" % u, [P, Q, PACK], BF16) for u in range(3)]
+        q_codes = [sbuf("q_codes%d" % u, [P, Q], U32) for u in range(3)]
+        q_sc = [sbuf("q_sc%d" % u, [P, Q], U8) for u in range(3)]
+
+        def cast_q(u):
+            nc.scalar.copy(q_bf[u][:].rearrange("p (c i) j -> p c j i", i=4),
+                           q_raw[u][:].rearrange("p j (c i) -> p c j i", i=4))
+
+        def quant_q(u):
+            nc.vector.quantize_mx(out=q_codes[u][:].bitcast(FP8X4), scales=q_sc[u][:],
+                                  in_=q_bf[u][:].rearrange("p q j -> p (q j)"))
+
+        zh = [bank("zh%d" % t, "z%d" % t) for t in range(PACK)]
+        cast_q(0)
+        cast_q(1)
+        hsc4 = sbuf("hsc4", [P, PACK], F32, "q_raw0")
+        nc.scalar.mul(hsc4[:], hsc_t[:], 4.0)
+        ht = [sbuf("ht%d" % h, [P, GROUP, RUNS, PACK, RUN], F32, ("q_raw1", "")[h]) for h in range(HALVES)]
+        for h in range(HALVES):
+            cols = slice(h * HALF, (h + 1) * HALF)
+            for t in range(PACK):
+                mc = slice(t * P, (t + 1) * P)
+                nc.tensor.matmul_mx(out=zh[t][:, cols], lhsT=w_codes[:, mc].bitcast(FP8X4), lhsT_scale=w_sc[:, mc],
+                                    rhs=tab_g[:, cols].bitcast(FP4X4), rhs_scale=tab_sc[:, cols], start=True, stop=True)
+            for t in range(PACK):
+                nc.scalar.activation(ht[h][:, :, :, t, :],
+                                     zh[t][:, cols].rearrange("p (a l j) -> p j a l", l=RUN, j=GROUP),
+                                     ACT.Exp, scale=temper_t[:, t:t + 1])
+
+        keys_sc = sbuf("keys_sc", [P, I], U8, "w_bf")
+        keys_g = sbuf("keys_g", [P, I], U16)
+        nc.vector.tensor_copy(keys_sc[:], keys_plane[:].indirect(offsets[:]))
+        nc.vector.tensor_copy(keys_g[:], keys_pool[:].indirect(offsets[:]))
+        quant_q(0)
+        quant_q(1)
+        cast_q(2)
+
+        sums = [bank("sum0", "s"), bank("sum1", "z0")]
+        rec_t = [sbuf("rec_t0", [P, P], F32, "keys_pool"), sbuf("rec_t1", [P, P], F32)]
+        factor = [sbuf("factor%d" % h, [P, RUNS, PACK, RUN], F32) for h in range(HALVES)]
+        hs_bf = [sbuf("hs_bf%d" % h, [P, GROUP, RUNS, RUN, PACK], BF16) for h in range(HALVES)]
+        hs_codes = [sbuf("hs_codes%d" % h, [P, HALF], U32) for h in range(HALVES)]
+        hs_sc = [sbuf("hs_sc%d" % h, [P, HALF], U8) for h in range(HALVES)]
+        back_tags = ("c", "z1")
+        c0_tags = ("s", "z2")
+
+        def group_sums(h):
+            for j in range(GROUP):
+                nc.tensor.matmul(sums[h][:, 0:P], ht[h][:, j].rearrange("p a t l -> p (a t l)"), identity[:],
+                                 start=(j == 0), stop=(j == GROUP - 1), is_transpose=True)
+
+        def reciprocals(h):
+            nc.vector.reciprocal(rec_t[h][:], sums[h][:, 0:P])
+            back = bank("back%d" % h, back_tags[h])
+            nc.tensor.transpose(back[:, 0:P], rec_t[h][:], identity[:])
+            return back
+
+        def factors(h, back):
+            nc.vector.tensor_tensor(factor[h][:], back[:, 0:P].rearrange("p (a t l) -> p a t l", t=PACK, l=RUN),
+                                    hsc4[:].unsqueeze(1).unsqueeze(3).broadcast_to([P, RUNS, PACK, RUN]), ALU.mult)
+
+        def normalise(h):
+            nc.vector.tensor_tensor(hs_bf[h][:].rearrange("p j a l t -> p j a t l"), ht[h][:],
+                                    factor[h][:].unsqueeze(1).broadcast_to([P, GROUP, RUNS, PACK, RUN]), ALU.mult)
+
+        def product(h):
+            nc.vector.quantize_mx(out=hs_codes[h][:].bitcast(FP8X4), scales=hs_sc[h][:],
+                                  in_=hs_bf[h][:].rearrange("p j a l t -> p (j a l t)"))
+            c0 = bank("c0_%d" % h, c0_tags[h])
+            nc.tensor.matmul_mx(out=c0[:, 0:HALF], lhsT=q_codes[2][:].bitcast(FP8X4), lhsT_scale=q_sc[2][:],
+                                rhs=hs_codes[h][:].bitcast(FP8X4), rhs_scale=hs_sc[h][:], start=True, stop=True)
+            return c0
+
+        group_sums(0)
+        score_a = bank("score_a", "a")
+        score_b = bank("score_b", "b")
+        for u, score in ((0, score_a), (1, score_b)):
+            nc.tensor.matmul_mx(out=score[:], lhsT=q_codes[u][:].bitcast(FP8X4), lhsT_scale=q_sc[u][:],
+                                rhs=keys_g[:].bitcast(FP4X4), rhs_scale=keys_sc[:], start=True, stop=True)
+        group_sums(1)
+        back0 = reciprocals(0)
+        neg_max = sbuf("neg_max", [P, 1], F32)
+        nc.vector.tensor_reduce(neg_max[:], score_a[:], AX.X, ALU.max, negate=True)
+        expo = sbuf("expo", [P, I], F32)
+        nc.scalar.activation(expo[:], score_a[:], ACT.Exp, bias=neg_max[:])
+        gate = sbuf("gate", [P, I], F32, "neg_max")
+        nc.scalar.activation(gate[:], score_b[:], ACT.Sigmoid)
+        factors(0, back0)
+        back1 = reciprocals(1)
+        quant_q(2)
+        normalise(0)
+        factors(1, back1)
+        c0_0 = product(0)
+        weight = sbuf("weight", [P, I], F32)
+        z = sbuf("z", [P, 1], F32)
+        nc.vector.scalar_tensor_tensor(weight[:], expo[:], 1.0, gate[:], ALU.mult, ALU.mult, accum_out=z[:])
+        normalise(1)
+        rz = sbuf("rz", [P, 1], F32)
+        nc.vector.reciprocal(rz[:], z[:])
+        c0_1 = product(1)
+        rz512 = sbuf("rz512", [P, 1], F32)
+        nc.scalar.mul(rz512[:], rz[:], 512.0)
+        direct = sbuf("direct", [P, I], F32)
+        part = [sbuf("part%d" % h, [P, 1], F32) for h in range(HALVES)]
+        for h, c0 in ((0, c0_0), (1, c0_1)):
+            cols = slice(h * HALF, (h + 1) * HALF)
+            nc.vector.scalar_tensor_tensor(direct[:, cols].rearrange("p (g j) -> p g j", j=GROUP),
+                                           c0[:, 0:HALF].rearrange("p (j g) -> p g j", j=GROUP), rz512[:],
+                                           weight[:, cols].rearrange("p (g j) -> p g j", j=GROUP),
+                                           ALU.mult, ALU.mult, accum_out=part[h][:])
+        mean = sbuf("mean", [P, 1], F32)
+        nc.vector.tensor_scalar(mean[:], part[1][:], part[0][:], rz[:], ALU.add, ALU.mult)
+        through = sbuf("through", [P, I], F32)
+        nc.vector.tensor_scalar(through[:], weight[:], mean[:], -1.0, ALU.mult, ALU.mult)
+        nc.vector.tensor_tensor(placed[:].indirect(offsets[:]), direct[:], through[:], ALU.add)
+        start = 0
+        for width in STORE_WIDTHS:
+            cols = slice(start, start + width)
+            nc.vector.tensor_tensor(result[:, cols], result[:, cols], placed[:, cols], ALU.add)
+            nc.sync.dma_start(out=out[:, cols], in_=result[:, cols])
+            start = start + width

@@ -25,14 +25,14 @@ HALVES = 2
 HALF = I // HALVES
 RUN = 4
 RUNS = HALF // GROUP // RUN
-W_SCALAR = 24
-STORE_WIDTHS = (512, 512, 512, 512)
+W_PIECES = ((0, 48, 64), (64, 88, 128))
+STORE_WIDTHS = (256, 512, 512, 512, 256)
 
 
-def load_scale_rows(queue, plane, scales):
+def load_scale_rows(queues, plane, scales):
     rows = scales[0].bitcast(I32).rearrange("(q r) c -> r q c", r=PACK)
     for r in range(PACK):
-        queue.dma_start(out=plane[r:P:32, :].bitcast(I32), in_=rows[r])
+        queues[r].dma_start(out=plane[r:P:32, :].bitcast(I32), in_=rows[r])
 
 
 def tile_attend_blrshared_asked_kernel(tc, query, query2, keys_words, keys_scales, tab_words, tab_scales,
@@ -50,12 +50,14 @@ def tile_attend_blrshared_asked_kernel(tc, query, query2, keys_words, keys_scale
 
         offsets = sb.tile([P, I // 16], U16, name="offsets")
         tab_plane = sbuf("tab_plane", [P, T], U8)
+        keys_plane = sbuf("keys_plane", [P, T], U8)
         placed = sbuf("placed", [P, T], F32)
         nc.vector.memset(tab_plane[:].bitcast(I32), 0)
+        nc.vector.memset(keys_plane[:].bitcast(I32), 0)
         nc.vector.memset(placed[:], 0.0)
 
         w_rows = w1.rearrange("(p j) c -> p j c", j=PACK)
-        w_raw = [sbuf("w_raw%d" % u, [P, PACK, R // 2], F32) for u in range(2)]
+        w_raw = [sbuf("w_raw%d" % u, [P, PACK, PACK * (m2 - m0)], F32) for u, (m0, m1, m2) in enumerate(W_PIECES)]
         tab_pool = sbuf("tab_pool", [P, T], U16)
         keys_pool = sbuf("keys_pool", [P, T], U16)
         q_raw = [sbuf("q_raw%d" % u, [P, PACK, Q], F32) for u in range(3)]
@@ -64,40 +66,39 @@ def tile_attend_blrshared_asked_kernel(tc, query, query2, keys_words, keys_scale
         result = sbuf("result", [P, T], F32)
 
         nc.sync.dma_start(offsets[:], offs)
-        nc.sync.dma_start(out=w_raw[0][:], in_=w_rows[:, :, 0:R // 2])
-        load_scale_rows(nc.sync, tab_plane, tab_scales)
+        nc.gpsimd.dma_start(out=hsc_t[:], in_=hsc.rearrange("(p t) o -> p (t o)", t=PACK))
+        nc.gpsimd.dma_start(out=temper_t[:], in_=temper.rearrange("(p t) o -> p (t o)", t=PACK))
         nc.sync.dma_start(out=tab_pool[:].bitcast(I32), in_=tab_words[0].bitcast(I32))
-        nc.sync.dma_start(out=w_raw[1][:], in_=w_rows[:, :, R // 2:R])
+        load_scale_rows([nc.sync] * 4, tab_plane, tab_scales)
+        for u, (m0, m1, m2) in enumerate(W_PIECES):
+            nc.sync.dma_start(out=w_raw[u][:], in_=w_rows[:, :, PACK * m0:PACK * m2])
         nc.sync.dma_start(out=q_raw[0][:], in_=query.rearrange("(p j) q -> p j q", j=PACK))
-        nc.sync.dma_start(out=q_raw[1][:], in_=query2.rearrange("(p j) q -> p j q", j=PACK))
+        load_scale_rows([nc.sync] * 4, keys_plane, keys_scales)
         nc.sync.dma_start(out=keys_pool[:].bitcast(I32), in_=keys_words[0].bitcast(I32))
+        nc.sync.dma_start(out=q_raw[1][:], in_=query2.rearrange("(p j) q -> p j q", j=PACK))
         nc.sync.dma_start(out=q_raw[2][:], in_=gout.rearrange("(p j) q -> p j q", j=PACK))
         nc.sync.dma_start(out=result[:], in_=old)
-        nc.gpsimd.dma_start(out=temper_t[:], in_=temper.rearrange("(p t) o -> p (t o)", t=PACK))
-        nc.gpsimd.dma_start(out=hsc_t[:], in_=hsc.rearrange("(p t) o -> p (t o)", t=PACK))
 
         identity = sbuf("identity", [P, P], F32)
         make_identity(nc, identity[:])
 
-        w_bf = sbuf("w_bf", [P, PACK, P, PACK], BF16)
-        M2 = P // 2
-
-        def w_views(u, m0, m1):
-            return (w_bf[:, :, u * M2 + m0:u * M2 + m1, :].rearrange("p t m j -> p m t j"),
-                    w_raw[u][:, :, PACK * m0:PACK * m1].rearrange("p j (m t) -> p m t j", t=PACK))
-
-        nc.scalar.activation(*w_views(0, 0, M2), ACT.Copy)
-        keys_plane = sbuf("keys_plane", [P, T], U8, "w_raw0")
-        nc.gpsimd.memset(keys_plane[:].bitcast(I32), 0)
-        load_scale_rows(nc.scalar, keys_plane, keys_scales)
         tab_sc = sbuf("tab_sc", [P, I], U8)
         tab_g = sbuf("tab_g", [P, I], U16)
+        nc.vector.tensor_copy(tab_g[:], tab_pool[:].indirect(offsets[:]))
         nc.vector.tensor_copy(tab_sc[:], tab_plane[:].indirect(offsets[:]))
-        for h in range(HALVES):
-            nc.vector.tensor_copy(tab_g[:, h * HALF:(h + 1) * HALF],
-                                  tab_pool[:].indirect(offsets[:, h * HALF // 16:(h + 1) * HALF // 16]))
-        nc.scalar.activation(*w_views(1, 0, W_SCALAR), ACT.Copy)
-        nc.vector.tensor_copy(*w_views(1, W_SCALAR, M2))
+
+        hsc4 = sbuf("hsc4", [P, PACK], F32)
+        nc.scalar.mul(hsc4[:], hsc_t[:], 4.0)
+        w_bf = sbuf("w_bf", [P, PACK, P, PACK], BF16)
+
+        def w_views(u, ma, mb):
+            m0 = W_PIECES[u][0]
+            return (w_bf[:, :, ma:mb, :].rearrange("p t m j -> p m t j"),
+                    w_raw[u][:, :, PACK * (ma - m0):PACK * (mb - m0)].rearrange("p j (m t) -> p m t j", t=PACK))
+
+        for u, (m0, m1, m2) in enumerate(W_PIECES):
+            nc.scalar.activation(*w_views(u, m0, m1), ACT.Copy)
+            nc.vector.tensor_copy(*w_views(u, m1, m2))
         w_codes = sbuf("w_codes", [P, R], U32)
         w_sc = sbuf("w_sc", [P, R], U8)
         for t in range(PACK):
@@ -119,10 +120,7 @@ def tile_attend_blrshared_asked_kernel(tc, query, query2, keys_words, keys_scale
 
         zh = [bank("zh%d" % t, "z%d" % t) for t in range(PACK)]
         cast_q(0)
-        cast_q(1)
-        hsc4 = sbuf("hsc4", [P, PACK], F32, "q_raw0")
-        nc.scalar.mul(hsc4[:], hsc_t[:], 4.0)
-        ht = [sbuf("ht%d" % h, [P, GROUP, RUNS, PACK, RUN], F32, ("q_raw1", "")[h]) for h in range(HALVES)]
+        ht = [sbuf("ht%d" % h, [P, GROUP, RUNS, PACK, RUN], F32, ("q_raw0", "")[h]) for h in range(HALVES)]
         for h in range(HALVES):
             cols = slice(h * HALF, (h + 1) * HALF)
             for t in range(PACK):
@@ -137,76 +135,87 @@ def tile_attend_blrshared_asked_kernel(tc, query, query2, keys_words, keys_scale
         keys_sc = sbuf("keys_sc", [P, I], U8, "w_bf")
         keys_g = sbuf("keys_g", [P, I], U16)
         nc.vector.tensor_copy(keys_sc[:], keys_plane[:].indirect(offsets[:]))
-        nc.vector.tensor_copy(keys_g[:], keys_pool[:].indirect(offsets[:]))
         quant_q(0)
-        quant_q(1)
+        nc.vector.tensor_copy(keys_g[:], keys_pool[:].indirect(offsets[:]))
+        cast_q(1)
         cast_q(2)
 
-        sums = [bank("sum0", "s"), bank("sum1", "z0")]
-        rec_t = [sbuf("rec_t0", [P, P], F32, "keys_pool"), sbuf("rec_t1", [P, P], F32)]
-        factor = [sbuf("factor%d" % h, [P, RUNS, PACK, RUN], F32) for h in range(HALVES)]
-        hs_bf = [sbuf("hs_bf%d" % h, [P, GROUP, RUNS, RUN, PACK], BF16) for h in range(HALVES)]
+        sum_tags = ("s", "a")
+        rec_tags = ("keys_pool", "")
+        factor_tags = ("", "")
         hs_codes = [sbuf("hs_codes%d" % h, [P, HALF], U32) for h in range(HALVES)]
         hs_sc = [sbuf("hs_sc%d" % h, [P, HALF], U8) for h in range(HALVES)]
         back_tags = ("c", "z1")
         c0_tags = ("s", "z2")
 
         def group_sums(h):
+            sums = bank("sum%d" % h, sum_tags[h])
             for j in range(GROUP):
-                nc.tensor.matmul(sums[h][:, 0:P], ht[h][:, j].rearrange("p a t l -> p (a t l)"), identity[:],
+                nc.tensor.matmul(sums[:, 0:P], ht[h][:, j].rearrange("p a t l -> p (a t l)"), identity[:],
                                  start=(j == 0), stop=(j == GROUP - 1), is_transpose=True)
+            return sums
 
-        def reciprocals(h):
-            nc.vector.reciprocal(rec_t[h][:], sums[h][:, 0:P])
+        def scores(u, tag):
+            score = bank("score_" + tag, tag)
+            nc.tensor.matmul_mx(out=score[:], lhsT=q_codes[u][:].bitcast(FP8X4), lhsT_scale=q_sc[u][:],
+                                rhs=keys_g[:].bitcast(FP4X4), rhs_scale=keys_sc[:], start=True, stop=True)
+            return score
+
+        def reciprocals(h, sums):
+            rec_t = sbuf("rec_t%d" % h, [P, P], F32, rec_tags[h])
+            nc.vector.reciprocal(rec_t[:], sums[:, 0:P])
             back = bank("back%d" % h, back_tags[h])
-            nc.tensor.transpose(back[:, 0:P], rec_t[h][:], identity[:])
+            nc.tensor.transpose(back[:, 0:P], rec_t[:], identity[:])
             return back
 
         def factors(h, back):
-            nc.vector.tensor_tensor(factor[h][:], back[:, 0:P].rearrange("p (a t l) -> p a t l", t=PACK, l=RUN),
+            factor = sbuf("factor%d" % h, [P, RUNS, PACK, RUN], F32, factor_tags[h])
+            nc.vector.tensor_tensor(factor[:], back[:, 0:P].rearrange("p (a t l) -> p a t l", t=PACK, l=RUN),
                                     hsc4[:].unsqueeze(1).unsqueeze(3).broadcast_to([P, RUNS, PACK, RUN]), ALU.mult)
+            return factor
 
-        def normalise(h):
-            nc.vector.tensor_tensor(hs_bf[h][:].rearrange("p j a l t -> p j a t l"), ht[h][:],
-                                    factor[h][:].unsqueeze(1).broadcast_to([P, GROUP, RUNS, PACK, RUN]), ALU.mult)
+        def normalise(h, factor, tag):
+            hs_bf = sbuf("hs_bf%d" % h, [P, GROUP, RUNS, RUN, PACK], BF16, tag)
+            nc.vector.tensor_tensor(hs_bf[:].rearrange("p j a l t -> p j a t l"), ht[h][:],
+                                    factor[:].unsqueeze(1).broadcast_to([P, GROUP, RUNS, PACK, RUN]), ALU.mult)
+            return hs_bf
 
-        def product(h):
+        def product(h, hs_bf):
             nc.vector.quantize_mx(out=hs_codes[h][:].bitcast(FP8X4), scales=hs_sc[h][:],
-                                  in_=hs_bf[h][:].rearrange("p j a l t -> p (j a l t)"))
+                                  in_=hs_bf[:].rearrange("p j a l t -> p (j a l t)"))
             c0 = bank("c0_%d" % h, c0_tags[h])
             nc.tensor.matmul_mx(out=c0[:, 0:HALF], lhsT=q_codes[2][:].bitcast(FP8X4), lhsT_scale=q_sc[2][:],
                                 rhs=hs_codes[h][:].bitcast(FP8X4), rhs_scale=hs_sc[h][:], start=True, stop=True)
             return c0
 
-        group_sums(0)
-        score_a = bank("score_a", "a")
-        score_b = bank("score_b", "b")
-        for u, score in ((0, score_a), (1, score_b)):
-            nc.tensor.matmul_mx(out=score[:], lhsT=q_codes[u][:].bitcast(FP8X4), lhsT_scale=q_sc[u][:],
-                                rhs=keys_g[:].bitcast(FP4X4), rhs_scale=keys_sc[:], start=True, stop=True)
-        group_sums(1)
-        back0 = reciprocals(0)
+        sums0 = group_sums(0)
+        score_a = scores(0, "a")
+        back0 = reciprocals(0, sums0)
+        quant_q(1)
+        score_b = scores(1, "b")
+        neg_a = sbuf("neg_a", [P, I], F32, "q_bf1")
         neg_max = sbuf("neg_max", [P, 1], F32)
-        nc.vector.tensor_reduce(neg_max[:], score_a[:], AX.X, ALU.max, negate=True)
-        expo = sbuf("expo", [P, I], F32)
-        nc.scalar.activation(expo[:], score_a[:], ACT.Exp, bias=neg_max[:])
+        nc.vector.tensor_scalar(neg_a[:], score_a[:], -1.0, None, ALU.mult, ALU.min, accum_out=neg_max[:])
+        sums1 = group_sums(1)
+        expo = sbuf("expo", [P, I], F32, "q_raw2")
+        nc.scalar.activation(expo[:], neg_a[:], ACT.Exp, bias=neg_max[:], scale=-1.0)
         gate = sbuf("gate", [P, I], F32, "neg_max")
         nc.scalar.activation(gate[:], score_b[:], ACT.Sigmoid)
-        factors(0, back0)
-        back1 = reciprocals(1)
+        factor0 = factors(0, back0)
         quant_q(2)
-        normalise(0)
-        factors(1, back1)
-        c0_0 = product(0)
+        hs_bf0 = normalise(0, factor0, "q_bf2")
+        back1 = reciprocals(1, sums1)
+        c0_0 = product(0, hs_bf0)
         weight = sbuf("weight", [P, I], F32)
         z = sbuf("z", [P, 1], F32)
         nc.vector.scalar_tensor_tensor(weight[:], expo[:], 1.0, gate[:], ALU.mult, ALU.mult, accum_out=z[:])
-        normalise(1)
-        rz = sbuf("rz", [P, 1], F32)
-        nc.vector.reciprocal(rz[:], z[:])
-        c0_1 = product(1)
+        factor1 = factors(1, back1)
+        z512 = sbuf("z512", [P, 1], F32)
+        nc.vector.tensor_scalar(z512[:], z[:], 1.0 / 512.0, None, ALU.mult)
+        hs_bf1 = normalise(1, factor1, "q_raw2")
         rz512 = sbuf("rz512", [P, 1], F32)
-        nc.scalar.mul(rz512[:], rz[:], 512.0)
+        nc.vector.reciprocal(rz512[:], z512[:])
+        c0_1 = product(1, hs_bf1)
         direct = sbuf("direct", [P, I], F32)
         part = [sbuf("part%d" % h, [P, 1], F32) for h in range(HALVES)]
         for h, c0 in ((0, c0_0), (1, c0_1)):
@@ -216,9 +225,9 @@ def tile_attend_blrshared_asked_kernel(tc, query, query2, keys_words, keys_scale
                                            weight[:, cols].rearrange("p (g j) -> p g j", j=GROUP),
                                            ALU.mult, ALU.mult, accum_out=part[h][:])
         mean = sbuf("mean", [P, 1], F32)
-        nc.vector.tensor_scalar(mean[:], part[1][:], part[0][:], rz[:], ALU.add, ALU.mult)
+        nc.vector.tensor_scalar(mean[:], part[1][:], part[0][:], rz512[:], ALU.add, ALU.mult)
         through = sbuf("through", [P, I], F32)
-        nc.vector.tensor_scalar(through[:], weight[:], mean[:], -1.0, ALU.mult, ALU.mult)
+        nc.vector.tensor_scalar(through[:], weight[:], mean[:], -1.0 / 512.0, ALU.mult, ALU.mult)
         nc.vector.tensor_tensor(placed[:].indirect(offsets[:]), direct[:], through[:], ALU.add)
         start = 0
         for width in STORE_WIDTHS:

@@ -66,15 +66,15 @@ def tile_attend_blrshared_asked_kernel(tc, query, query2, keys_words, keys_scale
         result = sbuf("result", [P, T], F32)
 
         nc.sync.dma_start(offsets[:], offs)
-        nc.gpsimd.dma_start(out=hsc_t[:], in_=hsc.rearrange("(p t) o -> p (t o)", t=PACK))
-        nc.gpsimd.dma_start(out=temper_t[:], in_=temper.rearrange("(p t) o -> p (t o)", t=PACK))
         nc.sync.dma_start(out=tab_pool[:].bitcast(I32), in_=tab_words[0].bitcast(I32))
         load_scale_rows([nc.sync] * 4, tab_plane, tab_scales)
         for u, (m0, m1, m2) in enumerate(W_PIECES):
             nc.sync.dma_start(out=w_raw[u][:], in_=w_rows[:, :, PACK * m0:PACK * m2])
+        nc.sync.dma_start(out=temper_t[:], in_=temper.rearrange("(p t) o -> p (t o)", t=PACK))
         nc.sync.dma_start(out=q_raw[0][:], in_=query.rearrange("(p j) q -> p j q", j=PACK))
         load_scale_rows([nc.sync] * 4, keys_plane, keys_scales)
         nc.sync.dma_start(out=keys_pool[:].bitcast(I32), in_=keys_words[0].bitcast(I32))
+        nc.sync.dma_start(out=hsc_t[:], in_=hsc.rearrange("(p t) o -> p (t o)", t=PACK))
         nc.sync.dma_start(out=q_raw[1][:], in_=query2.rearrange("(p j) q -> p j q", j=PACK))
         nc.sync.dma_start(out=q_raw[2][:], in_=gout.rearrange("(p j) q -> p j q", j=PACK))
         nc.sync.dma_start(out=result[:], in_=old)
@@ -87,8 +87,6 @@ def tile_attend_blrshared_asked_kernel(tc, query, query2, keys_words, keys_scale
         nc.vector.tensor_copy(tab_g[:], tab_pool[:].indirect(offsets[:]))
         nc.vector.tensor_copy(tab_sc[:], tab_plane[:].indirect(offsets[:]))
 
-        hsc4 = sbuf("hsc4", [P, PACK], F32)
-        nc.scalar.mul(hsc4[:], hsc_t[:], 4.0)
         w_bf = sbuf("w_bf", [P, PACK, P, PACK], BF16)
 
         def w_views(u, ma, mb):
@@ -137,12 +135,14 @@ def tile_attend_blrshared_asked_kernel(tc, query, query2, keys_words, keys_scale
         nc.vector.tensor_copy(keys_sc[:], keys_plane[:].indirect(offsets[:]))
         quant_q(0)
         nc.vector.tensor_copy(keys_g[:], keys_pool[:].indirect(offsets[:]))
+        hsc4 = sbuf("hsc4", [P, PACK], F32)
+        nc.scalar.mul(hsc4[:], hsc_t[:], 4.0)
         cast_q(1)
         cast_q(2)
 
         sum_tags = ("s", "a")
         rec_tags = ("keys_pool", "")
-        factor_tags = ("", "")
+        factor_tags = ("q_bf1", "")
         hs_codes = [sbuf("hs_codes%d" % h, [P, HALF], U32) for h in range(HALVES)]
         hs_sc = [sbuf("hs_sc%d" % h, [P, HALF], U8) for h in range(HALVES)]
         back_tags = ("c", "z1")
@@ -193,7 +193,7 @@ def tile_attend_blrshared_asked_kernel(tc, query, query2, keys_words, keys_scale
         back0 = reciprocals(0, sums0)
         quant_q(1)
         score_b = scores(1, "b")
-        neg_a = sbuf("neg_a", [P, I], F32, "q_bf1")
+        neg_a = sbuf("neg_a", [P, I], F32, "q_raw1")
         neg_max = sbuf("neg_max", [P, 1], F32)
         nc.vector.tensor_scalar(neg_a[:], score_a[:], -1.0, None, ALU.mult, ALU.min, accum_out=neg_max[:])
         sums1 = group_sums(1)

@@ -25,7 +25,7 @@ HALVES = 2
 HALF = I // HALVES
 RUN = 4
 RUNS = HALF // GROUP // RUN
-W_PIECES = ((0, 48, 64), (64, 88, 128))
+W_PIECES = ((0, 40, 64), (64, 82, 128))
 STORE_WIDTHS = (256, 512, 512, 512, 256)
 
 
@@ -116,18 +116,21 @@ def tile_attend_blrshared_asked_kernel(tc, query, query2, keys_words, keys_scale
             nc.vector.quantize_mx(out=q_codes[u][:].bitcast(FP8X4), scales=q_sc[u][:],
                                   in_=q_bf[u][:].rearrange("p q j -> p (q j)"))
 
-        zh = [bank("zh%d" % t, "z%d" % t) for t in range(PACK)]
+        zh_banks = [bank("zh%d" % n, tag) for n, tag in enumerate(("z0", "z1", "z2", "z3", "b", "c"))]
+        zh = [[zh_banks[t][:, 0:HALF] for t in range(PACK)],
+              [zh_banks[PACK + t // 2][:, (t % 2) * HALF:(t % 2 + 1) * HALF] for t in range(PACK)]]
         cast_q(0)
         ht = [sbuf("ht%d" % h, [P, GROUP, RUNS, PACK, RUN], F32, ("q_raw0", "")[h]) for h in range(HALVES)]
         for h in range(HALVES):
             cols = slice(h * HALF, (h + 1) * HALF)
             for t in range(PACK):
                 mc = slice(t * P, (t + 1) * P)
-                nc.tensor.matmul_mx(out=zh[t][:, cols], lhsT=w_codes[:, mc].bitcast(FP8X4), lhsT_scale=w_sc[:, mc],
+                nc.tensor.matmul_mx(out=zh[h][t], lhsT=w_codes[:, mc].bitcast(FP8X4), lhsT_scale=w_sc[:, mc],
                                     rhs=tab_g[:, cols].bitcast(FP4X4), rhs_scale=tab_sc[:, cols], start=True, stop=True)
+        for h in range(HALVES):
             for t in range(PACK):
                 nc.scalar.activation(ht[h][:, :, :, t, :],
-                                     zh[t][:, cols].rearrange("p (a l j) -> p j a l", l=RUN, j=GROUP),
+                                     zh[h][t].rearrange("p (a l j) -> p j a l", l=RUN, j=GROUP),
                                      ACT.Exp, scale=temper_t[:, t:t + 1])
 
         keys_sc = sbuf("keys_sc", [P, I], U8, "w_bf")
@@ -145,8 +148,8 @@ def tile_attend_blrshared_asked_kernel(tc, query, query2, keys_words, keys_scale
         factor_tags = ("q_bf1", "")
         hs_codes = [sbuf("hs_codes%d" % h, [P, HALF], U32) for h in range(HALVES)]
         hs_sc = [sbuf("hs_sc%d" % h, [P, HALF], U8) for h in range(HALVES)]
-        back_tags = ("c", "z1")
-        c0_tags = ("s", "z2")
+        back_tags = ("z0", "z1")
+        c0_tags = ("z2", "z3")
 
         def group_sums(h):
             sums = bank("sum%d" % h, sum_tags[h])

from contextlib import ExitStack

import concourse.mybir as mybir
from concourse.masks import make_identity

D, K, R, T, I, Q = 512, 512, 512, 2048, 512, 128
FLOPS = 2 * I * (2 * D * Q + K * R + R * Q)

F32 = mybir.dt.float32
BF16 = mybir.dt.bfloat16
I32 = mybir.dt.int32
U32 = mybir.dt.uint32
U16 = mybir.dt.uint16
U8 = mybir.dt.uint8
FP8X4 = mybir.dt.float8_e4m3fn_x4
FP4X4 = mybir.dt.float4_e2m1fn_x4
ALU = mybir.AluOpType
ACT = mybir.ActivationFunctionType
AX = mybir.AxisListType

P = 128
PACK = 4
GROUP = 8
HALVES = 2
HALF = I // HALVES
RUN = 4
RUNS = HALF // GROUP // RUN
W_PIECES = ((0, 40, 64), (64, 82, 128))
STORE_WIDTHS = (256, 512, 512, 512, 256)


def load_scale_rows(queues, plane, scales):
    rows = scales[0].bitcast(I32).rearrange("(q r) c -> r q c", r=PACK)
    for r in range(PACK):
        queues[r].dma_start(out=plane[r:P:32, :].bitcast(I32), in_=rows[r])


def tile_attend_blrshared_asked_kernel(tc, query, query2, keys_words, keys_scales, tab_words, tab_scales,
                                        w1, temper, gout, hsc, old, offs, out):
    nc = tc.nc
    with ExitStack() as ctx:
        sb = ctx.enter_context(tc.tile_pool(name="sb", bufs=1))
        ps = ctx.enter_context(tc.psum_pool(name="ps", bufs=1))

        def sbuf(name, shape, dtype, tag=""):
            return sb.tile(shape, dtype, name=name, tag=tag or name, align_bytes=64)

        def bank(name, tag):
            return ps.tile([P, 512], F32, name=name, tag=tag)

        offsets = sb.tile([P, I // 16], U16, name="offsets")
        tab_plane = sbuf("tab_plane", [P, T], U8)
        keys_plane = sbuf("keys_plane", [P, T], U8)
        placed = sbuf("placed", [P, T], F32)
        nc.vector.memset(tab_plane[:].bitcast(I32), 0)
        nc.vector.memset(keys_plane[:].bitcast(I32), 0)
        nc.vector.memset(placed[:], 0.0)

        w_rows = w1.rearrange("(p j) c -> p j c", j=PACK)
        w_raw = [sbuf("w_raw%d" % u, [P, PACK, PACK * (m2 - m0)], F32) for u, (m0, m1, m2) in enumerate(W_PIECES)]
        tab_pool = sbuf("tab_pool", [P, T], U16)
        keys_pool = sbuf("keys_pool", [P, T], U16)
        q_raw = [sbuf("q_raw%d" % u, [P, PACK, Q], F32) for u in range(3)]
        temper_t = sbuf("temper_t", [P, PACK], F32)
        hsc_t = sbuf("hsc_t", [P, PACK], F32)
        result = sbuf("result", [P, T], F32)

        nc.sync.dma_start(offsets[:], offs)
        nc.sync.dma_start(out=tab_pool[:].bitcast(I32), in_=tab_words[0].bitcast(I32))
        load_scale_rows([nc.sync] * 4, tab_plane, tab_scales)
        for u, (m0, m1, m2) in enumerate(W_PIECES):
            nc.sync.dma_start(out=w_raw[u][:], in_=w_rows[:, :, PACK * m0:PACK * m2])
        nc.sync.dma_start(out=temper_t[:], in_=temper.rearrange("(p t) o -> p (t o)", t=PACK))
        nc.sync.dma_start(out=q_raw[0][:], in_=query.rearrange("(p j) q -> p j q", j=PACK))
        load_scale_rows([nc.sync] * 4, keys_plane, keys_scales)
        nc.sync.dma_start(out=keys_pool[:].bitcast(I32), in_=keys_words[0].bitcast(I32))
        nc.sync.dma_start(out=hsc_t[:], in_=hsc.rearrange("(p t) o -> p (t o)", t=PACK))
        nc.sync.dma_start(out=q_raw[1][:], in_=query2.rearrange("(p j) q -> p j q", j=PACK))
        nc.sync.dma_start(out=q_raw[2][:], in_=gout.rearrange("(p j) q -> p j q", j=PACK))
        nc.sync.dma_start(out=result[:], in_=old)

        identity = sbuf("identity", [P, P], F32)
        make_identity(nc, identity[:])

        tab_sc = sbuf("tab_sc", [P, I], U8)
        tab_g = sbuf("tab_g", [P, I], U16)
        nc.vector.tensor_copy(tab_g[:], tab_pool[:].indirect(offsets[:]))
        nc.vector.tensor_copy(tab_sc[:], tab_plane[:].indirect(offsets[:]))

        w_bf = sbuf("w_bf", [P, PACK, P, PACK], BF16)

        def w_views(u, ma, mb):
            m0 = W_PIECES[u][0]
            return (w_bf[:, :, ma:mb, :].rearrange("p t m j -> p m t j"),
                    w_raw[u][:, :, PACK * (ma - m0):PACK * (mb - m0)].rearrange("p j (m t) -> p m t j", t=PACK))

        for u, (m0, m1, m2) in enumerate(W_PIECES):
            nc.scalar.activation(*w_views(u, m0, m1), ACT.Copy)
            nc.vector.tensor_copy(*w_views(u, m1, m2))
        w_codes = sbuf("w_codes", [P, R], U32)
        w_sc = sbuf("w_sc", [P, R], U8)
        for t in range(PACK):
            mc = slice(t * P, (t + 1) * P)
            nc.vector.quantize_mx(out=w_codes[:, mc].bitcast(FP8X4), scales=w_sc[:, mc],
                                  in_=w_bf[:, t].rearrange("p m j -> p (m j)"))

        q_bf = [sbuf("q_bf%d" % u, [P, Q, PACK], BF16) for u in range(3)]
        q_codes = [sbuf("q_codes%d" % u, [P, Q], U32) for u in range(3)]
        q_sc = [sbuf("q_sc%d" % u, [P, Q], U8) for u in range(3)]

        def cast_q(u):
            nc.scalar.copy(q_bf[u][:].rearrange("p (c i) j -> p c j i", i=4),
                           q_raw[u][:].rearrange("p j (c i) -> p c j i", i=4))

        def quant_q(u):
            nc.vector.quantize_mx(out=q_codes[u][:].bitcast(FP8X4), scales=q_sc[u][:],
                                  in_=q_bf[u][:].rearrange("p q j -> p (q j)"))

        zh_banks = [bank("zh%d" % n, tag) for n, tag in enumerate(("z0", "z1", "z2", "z3", "b", "c"))]
        zh = [[zh_banks[t][:, 0:HALF] for t in range(PACK)],
              [zh_banks[PACK + t // 2][:, (t % 2) * HALF:(t % 2 + 1) * HALF] for t in range(PACK)]]
        cast_q(0)
        ht = [sbuf("ht%d" % h, [P, GROUP, RUNS, PACK, RUN], F32, ("q_raw0", "")[h]) for h in range(HALVES)]
        for h in range(HALVES):
            cols = slice(h * HALF, (h + 1) * HALF)
            for t in range(PACK):
                mc = slice(t * P, (t + 1) * P)
                nc.tensor.matmul_mx(out=zh[h][t], lhsT=w_codes[:, mc].bitcast(FP8X4), lhsT_scale=w_sc[:, mc],
                                    rhs=tab_g[:, cols].bitcast(FP4X4), rhs_scale=tab_sc[:, cols], start=True, stop=True)
        for h in range(HALVES):
            for t in range(PACK):
                nc.scalar.activation(ht[h][:, :, :, t, :],
                                     zh[h][t].rearrange("p (a l j) -> p j a l", l=RUN, j=GROUP),
                                     ACT.Exp, scale=temper_t[:, t:t + 1])

        keys_sc = sbuf("keys_sc", [P, I], U8, "w_bf")
        keys_g = sbuf("keys_g", [P, I], U16)
        nc.vector.tensor_copy(keys_sc[:], keys_plane[:].indirect(offsets[:]))
        quant_q(0)
        nc.vector.tensor_copy(keys_g[:], keys_pool[:].indirect(offsets[:]))
        hsc4 = sbuf("hsc4", [P, PACK], F32)
        nc.scalar.mul(hsc4[:], hsc_t[:], 4.0)
        cast_q(1)
        cast_q(2)

        sum_tags = ("s", "a")
        rec_tags = ("keys_pool", "")
        factor_tags = ("q_bf1", "")
        hs_codes = [sbuf("hs_codes%d" % h, [P, HALF], U32) for h in range(HALVES)]
        hs_sc = [sbuf("hs_sc%d" % h, [P, HALF], U8) for h in range(HALVES)]
        back_tags = ("z0", "z1")
        c0_tags = ("z2", "z3")

        def group_sums(h):
            sums = bank("sum%d" % h, sum_tags[h])
            for j in range(GROUP):
                nc.tensor.matmul(sums[:, 0:P], ht[h][:, j].rearrange("p a t l -> p (a t l)"), identity[:],
                                 start=(j == 0), stop=(j == GROUP - 1), is_transpose=True)
            return sums

        def scores(u, tag):
            score = bank("score_" + tag, tag)
            nc.tensor.matmul_mx(out=score[:], lhsT=q_codes[u][:].bitcast(FP8X4), lhsT_scale=q_sc[u][:],
                                rhs=keys_g[:].bitcast(FP4X4), rhs_scale=keys_sc[:], start=True, stop=True)
            return score

        def reciprocals(h, sums):
            rec_t = sbuf("rec_t%d" % h, [P, P], F32, rec_tags[h])
            nc.vector.reciprocal(rec_t[:], sums[:, 0:P])
            back = bank("back%d" % h, back_tags[h])
            nc.tensor.transpose(back[:, 0:P], rec_t[:], identity[:])
            return back

        def factors(h, back):
            factor = sbuf("factor%d" % h, [P, RUNS, PACK, RUN], F32, factor_tags[h])
            nc.vector.tensor_tensor(factor[:], back[:, 0:P].rearrange("p (a t l) -> p a t l", t=PACK, l=RUN),
                                    hsc4[:].unsqueeze(1).unsqueeze(3).broadcast_to([P, RUNS, PACK, RUN]), ALU.mult)
            return factor

        def normalise(h, factor, tag):
            hs_bf = sbuf("hs_bf%d" % h, [P, GROUP, RUNS, RUN, PACK], BF16, tag)
            nc.vector.tensor_tensor(hs_bf[:].rearrange("p j a l t -> p j a t l"), ht[h][:],
                                    factor[:].unsqueeze(1).broadcast_to([P, GROUP, RUNS, PACK, RUN]), ALU.mult)
            return hs_bf

        def product(h, hs_bf):
            nc.vector.quantize_mx(out=hs_codes[h][:].bitcast(FP8X4), scales=hs_sc[h][:],
                                  in_=hs_bf[:].rearrange("p j a l t -> p (j a l t)"))
            c0 = bank("c0_%d" % h, c0_tags[h])
            nc.tensor.matmul_mx(out=c0[:, 0:HALF], lhsT=q_codes[2][:].bitcast(FP8X4), lhsT_scale=q_sc[2][:],
                                rhs=hs_codes[h][:].bitcast(FP8X4), rhs_scale=hs_sc[h][:], start=True, stop=True)
            return c0

        sums0 = group_sums(0)
        score_a = scores(0, "a")
        back0 = reciprocals(0, sums0)
        quant_q(1)
        score_b = scores(1, "b")
        neg_a = sbuf("neg_a", [P, I], F32, "q_raw1")
        neg_max = sbuf("neg_max", [P, 1], F32)
        nc.vector.tensor_scalar(neg_a[:], score_a[:], -1.0, None, ALU.mult, ALU.min, accum_out=neg_max[:])
        sums1 = group_sums(1)
        expo = sbuf("expo", [P, I], F32, "q_raw2")
        nc.scalar.activation(expo[:], neg_a[:], ACT.Exp, bias=neg_max[:], scale=-1.0)
        gate = sbuf("gate", [P, I], F32, "neg_max")
        nc.scalar.activation(gate[:], score_b[:], ACT.Sigmoid)
        factor0 = factors(0, back0)
        quant_q(2)
        hs_bf0 = normalise(0, factor0, "q_bf2")
        back1 = reciprocals(1, sums1)
        c0_0 = product(0, hs_bf0)
        weight = sbuf("weight", [P, I], F32)
        z = sbuf("z", [P, 1], F32)
        nc.vector.scalar_tensor_tensor(weight[:], expo[:], 1.0, gate[:], ALU.mult, ALU.mult, accum_out=z[:])
        factor1 = factors(1, back1)
        z512 = sbuf("z512", [P, 1], F32)
        nc.vector.tensor_scalar(z512[:], z[:], 1.0 / 512.0, None, ALU.mult)
        hs_bf1 = normalise(1, factor1, "q_raw2")
        rz512 = sbuf("rz512", [P, 1], F32)
        nc.vector.reciprocal(rz512[:], z512[:])
        c0_1 = product(1, hs_bf1)
        direct = sbuf("direct", [P, I], F32)
        part = [sbuf("part%d" % h, [P, 1], F32) for h in range(HALVES)]
        for h, c0 in ((0, c0_0), (1, c0_1)):
            cols = slice(h * HALF, (h + 1) * HALF)
            nc.vector.scalar_tensor_tensor(direct[:, cols].rearrange("p (g j) -> p g j", j=GROUP),
                                           c0[:, 0:HALF].rearrange("p (j g) -> p g j", j=GROUP), rz512[:],
                                           weight[:, cols].rearrange("p (g j) -> p g j", j=GROUP),
                                           ALU.mult, ALU.mult, accum_out=part[h][:])
        mean = sbuf("mean", [P, 1], F32)
        nc.vector.tensor_scalar(mean[:], part[1][:], part[0][:], rz512[:], ALU.add, ALU.mult)
        through = sbuf("through", [P, I], F32)
        nc.vector.tensor_scalar(through[:], weight[:], mean[:], -1.0 / 512.0, ALU.mult, ALU.mult)
        nc.vector.tensor_tensor(placed[:].indirect(offsets[:]), direct[:], through[:], ALU.add)
        start = 0
        for width in STORE_WIDTHS:
            cols = slice(start, start + width)
            nc.vector.tensor_tensor(result[:, cols], result[:, cols], placed[:, cols], ALU.add)
            nc.sync.dma_start(out=out[:, cols], in_=result[:, cols])
            start = start + width
